import numpy as np
import ml_dtypes


def mxq(x, axis, fmt="e4m3"):
    dtype, down = {"e4m3": (ml_dtypes.float8_e4m3fn, 7), "e5m2": (ml_dtypes.float8_e5m2, 14)}[fmt]
    v = np.moveaxis(np.asarray(x, np.float32).astype(ml_dtypes.bfloat16).astype(np.float64), axis, -1)
    blocks = v.reshape(v.shape[:-1] + (-1, 32))
    amax = np.abs(blocks).max(-1, keepdims=True)
    byte = np.maximum(np.where(amax > 0, np.frexp(amax)[1] - 1 + 127, 0) - down, 1)
    scale = np.exp2(byte - 127.0)
    codes = (blocks / scale).astype(np.float32).astype(dtype).astype(np.float64)
    return np.moveaxis((codes * scale).reshape(v.shape), -1, axis)


WIDE = False


def mx_kscale(k):
    if not WIDE:
        return np.ones(k)
    levels = np.array([10, -10, 5, -5, 0])
    if k % 512:
        return np.exp2(np.random.permutation(np.resize(levels, k // 32))).repeat(32)
    a = np.empty((k // 512, 16))
    for p in range(k // 512):
        a[p, :8] = np.random.permutation(np.resize(levels, 8))
        for g in range(8):
            far = levels[np.abs(levels - a[p, g]) >= 10]
            a[p, g + 8] = far[np.random.randint(len(far))]
    return np.exp2(a.ravel()).repeat(32)


def f64(x):
    return np.asarray(x).astype(np.float64)


def striped8(idx):
    return np.concatenate([x.reshape(-1, 16).T for x in idx]).astype(np.uint16)


def runs(offs, k):
    lists = np.stack([offs[16 * r : 16 * r + 16].T.reshape(-1) for r in range(8)]).astype(np.int64)
    return lists[np.arange(k) % 512 // 64]


def pack_weight(w):
    k, n = w.shape
    w = f64(np.asarray(w, np.float32).astype(ml_dtypes.bfloat16)).reshape(k // 32, 32, n)
    amax = np.abs(w).max(1)
    byte = np.clip(np.where(amax > 0, np.frexp(amax)[1] - 1 + 127 - 7, 1), 1, 254)
    scaled = (w * np.exp2(127.0 - byte)[:, None, :]).reshape(k, n).astype(np.float32)
    words = np.ascontiguousarray(scaled.reshape(k // 512, 128, 4, n).transpose(0, 1, 3, 2)).astype(ml_dtypes.float8_e4m3fn).view(np.uint8)
    return words, np.ascontiguousarray(byte.astype(np.uint8).reshape(k // 512, 16, n))


def unpack_weight(words, scales):
    g, p, n, _ = words.shape
    vals = np.ascontiguousarray(words).view(ml_dtypes.float8_e4m3fn).astype(np.float64) * np.repeat(np.exp2(scales.astype(np.float64) - 127.0), 8, axis=1)[..., None]
    return vals.transpose(0, 1, 3, 2).reshape(g * 512, n)


def sigmoid(v):
    return 1.0 / (1.0 + np.exp(-np.maximum(v, -700.0)))

def planes(y):
    n, m = y.shape
    v = y.astype(np.float32).astype(ml_dtypes.bfloat16).astype(np.float64).reshape(n // 32, 32, m)
    top = np.abs(v).max(1)
    byte = np.clip(np.where(top > 0, np.frexp(top)[1] - 1 + 127 - 7, 1), 1, 254)
    codes = (v * np.exp2(127.0 - byte)[:, None, :]).reshape(n, m).astype(np.float32).astype(ml_dtypes.float8_e4m3fn).view(np.uint8)
    words = codes.reshape(n // 512, 128, 4, m).transpose(0, 1, 3, 2)
    return np.ascontiguousarray(words), np.ascontiguousarray(byte.astype(np.uint8).reshape(n // 512, 16, m))


K, T, S, N, H, W = 512, 2048, 512, 512, 512, 256


def setup_inputs():
    n = np.random.standard_normal
    s = mx_kscale(K)[:, None]
    u = mx_kscale(H)
    packed_xT = pack_weight(n((K, T)) * s)
    packed_w1 = pack_weight(n((K, H)) / np.sqrt(K) / s)
    packed_w2 = pack_weight(n((H, N)) / np.sqrt(H) / u[:, None])
    perm = np.stack([np.random.permutation(S) for _ in range(8)])
    return {
        "x_words": packed_xT[0],
        "x_scales": packed_xT[1],
        "w1_words": packed_w1[0],
        "w1_scales": packed_w1[1],
        "gn": (np.random.uniform(0.5, 1.5, (H, 1)) * u[:, None]).astype(np.float32),
        "w2_words": packed_w2[0],
        "w2_scales": packed_w2[1],
        "offs": striped8(np.random.randint(0, T, (8, S))),
        "n1": striped8(perm[:, :W]),
        "n2": striped8(perm[:, W:]),
        "n3": striped8(np.stack([np.random.permutation(S) for _ in range(8)])),
    }


def reference(x_words, x_scales, w1_words, w1_scales, gn, w2_words, w2_scales, offs, n1, n2, n3):
    xq = unpack_weight(x_words, x_scales)[np.arange(K)[:, None], runs(offs, K)]
    y = unpack_weight(w1_words, w1_scales).T @ xq
    pa = y[np.arange(H)[:, None], runs(n1, H)]
    pb = y[np.arange(H)[:, None], runs(n2, H)]
    ra = np.maximum(pa, pb)
    ds = y.copy()
    ds[np.arange(H)[:, None], runs(n1, H)] = ra
    z = f64(gn) * ds
    h = unpack_weight(w2_words, w2_scales).T @ mxq(z, 0, "e4m3")
    out_0 = h * (sigmoid(h[np.arange(N)[:, None], runs(n3, N)]))
    return (out_0,) + planes(out_0)

@@ -1,0 +1,201 @@
+from contextlib import ExitStack
+
+import concourse.mybir as mybir
+
+F32 = mybir.dt.float32
+BF16 = mybir.dt.bfloat16
+I32 = mybir.dt.int32
+U32 = mybir.dt.uint32
+U16 = mybir.dt.uint16
+U8 = mybir.dt.uint8
+FP8X4 = mybir.dt.float8_e4m3fn_x4
+ALU = mybir.AluOpType
+ACT = mybir.ActivationFunctionType
+
+P = 128
+PACK = 4
+T = 2048
+S = 512
+W = 256
+HALF = S // 2
+QUADS = 4
+FLOPS = 2 * 2 * 512 * 512 * 512
+
+
+def tile_picked_hashfillgate_none_po_kernel(
+    tc, x_words, x_scales, w1_words, w1_scales, gn, w2_words, w2_scales, offs, n1, n2, n3, out_0, out_1, out_2
+):
+    nc = tc.nc
+    with ExitStack() as ctx:
+        keep = ctx.enter_context(tc.tile_pool(name="keep", bufs=1))
+        psum = ctx.enter_context(tc.psum_pool(name="psum", bufs=1))
+
+        def words_view(dram):
+            return dram[0].rearrange("p n r -> p (n r)").bitcast(I32)
+
+        def entries(lst, lo, hi):
+            return lst[:, lo // 16 : hi // 16]
+
+        offs_sb = keep.tile([P, S // 16], U16, name="offs_sb")
+        n1_sb = keep.tile([P, W // 16], U16, name="n1_sb")
+        n2_sb = keep.tile([P, W // 16], U16, name="n2_sb")
+        n3_sb = keep.tile([P, S // 16], U16, name="n3_sb")
+        xs_table = keep.tile([P, T], U8, name="xs_table", align_bytes=64)
+        xw_table = keep.tile([P, T], I32, name="xw_table", align_bytes=64)
+        ws_raw = keep.tile([P, S], U8, name="ws_raw", align_bytes=64)
+        ww_raw = keep.tile([P, S], I32, name="ww_raw", align_bytes=64)
+        xs_plane = keep.tile([P, S], U8, name="xs_plane", align_bytes=64)
+        gn_sb = keep.tile([P, PACK], F32, name="gn_sb")
+        warm = keep.tile([P, 2], F32, name="warm")
+
+        nc.vector.memset(xs_table[:].bitcast(I32), 0)
+        nc.gpsimd.memset(ws_raw[:].bitcast(I32), 0)
+        nc.vector.memset(xs_plane[:].bitcast(I32), 0)
+        nc.vector.memset(warm[:, 0:1], 0.0)
+
+        def load_scales(dram, queues):
+            for q in range(QUADS):
+                queues[q].dma_start(ws_raw[32 * q : 32 * q + 4, :].bitcast(I32), dram[0, 4 * q : 4 * q + 4, :].bitcast(I32))
+
+        nc.sync.dma_start(offs_sb[:], offs)
+        nc.scalar.dma_start(xs_table[0:P:8, :].bitcast(I32), x_scales[0].bitcast(I32))
+        load_scales(w1_scales, [nc.gpsimd, nc.gpsimd, nc.scalar, nc.scalar])
+        nc.scalar.dma_start(ww_raw[:], words_view(w1_words))
+        nc.sync.dma_start(n1_sb[:], n1)
+        nc.sync.dma_start(n2_sb[:], n2)
+        nc.sync.dma_start(xw_table[:], words_view(x_words))
+        nc.sync.dma_start(n3_sb[:], n3)
+        nc.gpsimd.dma_start(gn_sb[:], gn.rearrange("(p t) o -> p (t o)", t=PACK))
+        nc.scalar.activation(warm[:, 1:2], warm[:, 0:1], ACT.Sigmoid)
+
+        xs_picked = keep.tile([P, S], U8, name="xs_picked", align_bytes=64)
+        nc.vector.tensor_copy(xs_picked[:], xs_table[:].indirect(offs_sb[:]))
+        for q in range(QUADS):
+            queue = nc.sync if q % 2 == 0 else nc.scalar
+            queue.dma_start(xs_plane[32 * q : 32 * q + 4, :].bitcast(I32), xs_picked[32 * q : 32 * q + 32 : 8, :].bitcast(I32))
+
+        def deal(name):
+            words = keep.tile([P, PACK, P], I32, name=name + "_words", align_bytes=64)
+            scales = keep.tile([P, PACK, P], U8, name=name + "_scales", align_bytes=64)
+            nc.vector.tensor_copy(scales[:], ws_raw[:].rearrange("p (m t) -> p t m", t=PACK))
+            nc.vector.tensor_copy(words[:], ww_raw[:].rearrange("p (m t) -> p t m", t=PACK))
+            return words, scales
+
+        w1w, w1s = deal("w1")
+        load_scales(w2_scales, [nc.sync] * QUADS)
+        nc.sync.dma_start(ww_raw[:], words_view(w2_words))
+
+        gain = keep.tile([P, PACK, W], F32, name="gain")
+
+        xw_picked = [keep.tile([P, HALF], U32, name=f"xw_picked{h}", align_bytes=64) for h in range(2)]
+        for h in range(2):
+            nc.vector.tensor_copy(
+                xw_picked[h][:],
+                xw_table[:].bitcast(U32).indirect(entries(offs_sb, h * HALF, (h + 1) * HALF)),
+            )
+
+        def product(dst, words, scales, t, rhs_words, rhs_scales):
+            nc.tensor.matmul_mx(
+                dst,
+                lhsT=words[:, t, :].bitcast(FP8X4),
+                lhsT_scale=scales[:, t, :],
+                rhs=rhs_words.bitcast(FP8X4),
+                rhs_scale=rhs_scales,
+                start=True,
+                stop=True,
+            )
+
+        halves = [slice(0, HALF), slice(HALF, S)]
+        order = (1, 3, 0, 2)
+        y_sb = {t: keep.tile([P, S], F32, name=f"y_sb{t}") for t in order}
+        z_sb = {t: keep.tile([P, S if t % 2 else 2 * S], F32, name=f"z_sb{t}") for t in order}
+        pieces = {t: (halves if t == order[0] else [slice(0, S)]) for t in order}
+        y_ps = {}
+        for t in order:
+            for i, cols in enumerate(pieces[t]):
+                y_ps[t, i] = psum.tile([P, cols.stop - cols.start], F32, name=f"y_ps{t}_{i}", tag=f"bank{t + 4 * i}")
+                for h in range(2):
+                    if halves[h].start >= cols.start and halves[h].stop <= cols.stop:
+                        lo = halves[h].start - cols.start
+                        product(y_ps[t, i][:, lo : lo + HALF], w1w, w1s, t, xw_picked[h][:], xs_plane[:, halves[h]])
+        w2w, w2s = deal("w2")
+
+        def fetch_y(t):
+            for i, cols in enumerate(pieces[t]):
+                nc.scalar.copy(y_sb[t][:, cols], y_ps[t, i][:])
+
+        def fetch_z(t):
+            for i, cols in enumerate(pieces[t]):
+                nc.scalar.activation(z_sb[t][:, cols], y_ps[t, i][:], ACT.Copy, scale=gn_sb[:, t : t + 1])
+            nc.scalar.activation(gain[:, t, :], gn_sb[:, t : t + 1].to_broadcast([P, W]), ACT.Copy)
+
+        pa = {t: keep.tile([P, W], F32, name=f"pa{t}") for t in order}
+        pb = {t: keep.tile([P, W], F32, name=f"pb{t}") for t in order}
+        ra = {t: keep.tile([P, W], F32, name=f"ra{t}") for t in order}
+        z_bf = [keep.tile([P, HALF, PACK], BF16, name=f"z_bf{h}", align_bytes=64) for h in range(2)]
+
+        def fill(t):
+            nc.vector.tensor_tensor(z_sb[t][:].indirect(n1_sb[:]), ra[t][:], gain[:, t, :], ALU.mult)
+            if t % 2:
+                nc.scalar.copy(z_sb[t - 1][:, S : 2 * S], z_sb[t][:])
+            else:
+                pair = z_sb[t][:].rearrange("p (e n) -> p n e", e=2)
+                for h in range(2):
+                    if t == 0:
+                        nc.scalar.copy(z_bf[h][:, :, t : t + 2], pair[:, halves[h], :])
+                    elif h == 0:
+                        nc.vector.tensor_copy(z_bf[h][:, :, t : t + 2], pair[:, halves[h], :])
+                    else:
+                        nc.vector.tensor_copy(z_bf[h][:, 0:SPLIT, t : t + 2], pair[:, HALF : HALF + SPLIT, :])
+                        nc.scalar.copy(z_bf[h][:, SPLIT:HALF, t : t + 2], pair[:, HALF + SPLIT : S, :])
+
+        SPLIT = 96
+        fetch_y(order[0])
+        for i, t in enumerate(order):
+            if i + 1 < PACK:
+                fetch_y(order[i + 1])
+            fetch_z(t)
+            nc.vector.tensor_copy(pa[t][:], y_sb[t][:].indirect(n1_sb[:]))
+            if i > 0:
+                prev = order[i - 1]
+                nc.vector.tensor_tensor(ra[prev][:], pa[prev][:], pb[prev][:], ALU.max)
+            nc.vector.tensor_copy(pb[t][:], y_sb[t][:].indirect(n2_sb[:]))
+            if i > 0 and i + 1 < PACK:
+                fill(order[i - 1])
+        nc.vector.tensor_tensor(ra[t][:], pa[t][:], pb[t][:], ALU.max)
+        fill(order[PACK - 2])
+        fill(order[PACK - 1])
+
+        z_words = keep.tile([P, S], U32, name="z_words", align_bytes=64)
+        z_scales = keep.tile([P, S], U8, name="z_scales", align_bytes=64)
+        h_ps = [psum.tile([P, S], F32, name=f"h_ps{t}", tag=f"bank{(t + 5) % 8}") for t in range(PACK)]
+        for h in range(2):
+            cols = halves[h]
+            nc.vector.quantize_mx(z_words[:, cols].bitcast(FP8X4), z_scales[:, cols], z_bf[h][:].rearrange("p n t -> p (n t)"))
+            product(h_ps[0][:, cols], w2w, w2s, 0, z_words[:, cols], z_scales[:, cols])
+        for t in range(1, PACK):
+            product(h_ps[t][:], w2w, w2s, t, z_words[:], z_scales[:])
+
+        h_sb = [keep.tile([P, S], F32, name=f"h_sb{t}") for t in range(PACK)]
+        for t in range(PACK):
+            nc.vector.tensor_copy(h_sb[t][:], h_ps[t][:])
+
+        out_rows = out_0.rearrange("(p t) n -> p t n", t=PACK)
+        o_scales = keep.tile([P, S], U8, name="o_scales", align_bytes=64)
+        chunks = [(0, 256), (256, 384), (384, 512)]
+        for c, (lo, hi) in enumerate(chunks):
+            cols = slice(lo, hi)
+            o_sb = keep.tile([P, PACK, hi - lo], F32, name=f"o_sb{c}")
+            for t in range(PACK):
+                gate = keep.tile([P, hi - lo], F32, name=f"gate{c}{t}")
+                nc.scalar.activation(gate[:], h_sb[t][:].indirect(entries(n3_sb, lo, hi)), ACT.Sigmoid)
+                nc.vector.tensor_tensor(o_sb[:, t, :], h_ps[t][:, cols], gate[:], ALU.mult)
+            nc.sync.dma_start(out_rows[:, :, cols], o_sb[:])
+            o_bf = keep.tile([P, hi - lo, PACK], BF16, name=f"o_bf{c}", align_bytes=64)
+            nc.vector.tensor_copy(o_bf[:], o_sb[:].rearrange("p t n -> p n t"))
+            o_words = keep.tile([P, hi - lo], I32, name=f"o_words{c}", align_bytes=64)
+            nc.vector.quantize_mx(o_words[:].bitcast(FP8X4), o_scales[:, cols], o_bf[:].rearrange("p n t -> p (n t)"))
+            nc.sync.dma_start(words_view(out_1)[:, cols], o_words[:])
+        for q in range(QUADS):
+            queue = nc.sync if q % 2 == 0 else nc.scalar
+            queue.dma_start(out_2[0, 4 * q : 4 * q + 4, :].bitcast(I32), o_scales[32 * q : 32 * q + 4, :].bitcast(I32))

@@ -42,50 +42,59 @@ def tile_picked_hashfillgate_none_po_kernel(
         n3_sb = keep.tile([P, S // 16], U16, name="n3_sb")
         xs_table = keep.tile([P, T], U8, name="xs_table", align_bytes=64)
         xw_table = keep.tile([P, T], I32, name="xw_table", align_bytes=64)
-        ws_raw = keep.tile([P, S], U8, name="ws_raw", align_bytes=64)
-        ww_raw = keep.tile([P, S], I32, name="ww_raw", align_bytes=64)
-        xs_plane = keep.tile([P, S], U8, name="xs_plane", align_bytes=64)
+        w1s_raw = keep.tile([P, S], U8, name="w1s_raw", align_bytes=64)
+        w2s_raw = keep.tile([P, S], U8, name="w2s_raw", align_bytes=64)
+        w1w_raw = keep.tile([P, S], I32, name="w1w_raw", align_bytes=64)
+        w2w_raw = keep.tile([P, S], I32, name="w2w_raw", align_bytes=64)
+        planes1 = keep.tile([P, 3 * S], U8, name="planes1", align_bytes=64)
         gn_sb = keep.tile([P, PACK], F32, name="gn_sb")
         warm = keep.tile([P, 2], F32, name="warm")
 
-        nc.vector.memset(xs_table[:].bitcast(I32), 0)
-        nc.gpsimd.memset(ws_raw[:].bitcast(I32), 0)
-        nc.vector.memset(xs_plane[:].bitcast(I32), 0)
+        def repeated(dram):
+            rows = dram[0].bitcast(I32)
+            return rows.unsqueeze(1).to_broadcast([16, 8, rows.shape[1]])
+
+        nc.vector.memset(planes1[:].bitcast(I32), 0)
         nc.vector.memset(warm[:, 0:1], 0.0)
 
-        def load_scales(dram, queues):
-            for q in range(QUADS):
-                queues[q].dma_start(ws_raw[32 * q : 32 * q + 4, :].bitcast(I32), dram[0, 4 * q : 4 * q + 4, :].bitcast(I32))
-
+        nc.sync.dma_start(w1s_raw[:].bitcast(I32), repeated(w1_scales))
+        nc.sync.dma_start(w2s_raw[:].bitcast(I32), repeated(w2_scales))
         nc.sync.dma_start(offs_sb[:], offs)
-        nc.scalar.dma_start(xs_table[0:P:8, :].bitcast(I32), x_scales[0].bitcast(I32))
-        load_scales(w1_scales, [nc.gpsimd, nc.gpsimd, nc.scalar, nc.scalar])
-        nc.scalar.dma_start(ww_raw[:], words_view(w1_words))
+        nc.sync.dma_start(xs_table[:].bitcast(I32), repeated(x_scales))
         nc.sync.dma_start(n1_sb[:], n1)
         nc.sync.dma_start(n2_sb[:], n2)
+        nc.sync.dma_start(gn_sb[:], gn.rearrange("(p t) o -> p (t o)", t=PACK))
         nc.sync.dma_start(xw_table[:], words_view(x_words))
+        nc.sync.dma_start(w1w_raw[:], words_view(w1_words))
         nc.sync.dma_start(n3_sb[:], n3)
-        nc.gpsimd.dma_start(gn_sb[:], gn.rearrange("(p t) o -> p (t o)", t=PACK))
+        nc.sync.dma_start(w2w_raw[:], words_view(w2_words))
         nc.scalar.activation(warm[:, 1:2], warm[:, 0:1], ACT.Sigmoid)
 
+        def dealt(raw):
+            return raw[:].rearrange("p (m t) -> p t m", t=PACK)
+
+        def move_rows(dst, src, queues):
+            for q in range(QUADS):
+                queues[q].dma_start(dst[32 * q : 32 * q + 4, :].bitcast(I32), src[32 * q : 32 * q + 32 : 8, :].bitcast(I32))
+
+        rows1 = keep.tile([P, 3 * S], U8, name="rows1", align_bytes=64)
+        nc.vector.tensor_copy(rows1[:, S : 2 * S].rearrange("p (t m) -> p t m", t=PACK), dealt(w1s_raw))
+        nc.gpsimd.tensor_copy(rows1[:, 2 * S : 3 * S].rearrange("p (t m) -> p t m", t=PACK), dealt(w2s_raw))
         xs_picked = keep.tile([P, S], U8, name="xs_picked", align_bytes=64)
         nc.vector.tensor_copy(xs_picked[:], xs_table[:].indirect(offs_sb[:]))
-        for q in range(QUADS):
-            queue = nc.sync if q % 2 == 0 else nc.scalar
-            queue.dma_start(xs_plane[32 * q : 32 * q + 4, :].bitcast(I32), xs_picked[32 * q : 32 * q + 32 : 8, :].bitcast(I32))
+        nc.vector.tensor_copy(rows1[:, 0:S].bitcast(I32), xs_picked[:].bitcast(I32))
+        move_rows(planes1, rows1, [nc.sync, nc.scalar, nc.sync, nc.scalar])
+        xs_plane = planes1[:, 0:S]
+        w1s = planes1[:, S : 2 * S]
 
-        def deal(name):
-            words = keep.tile([P, PACK, P], I32, name=name + "_words", align_bytes=64)
-            scales = keep.tile([P, PACK, P], U8, name=name + "_scales", align_bytes=64)
-            nc.vector.tensor_copy(scales[:], ws_raw[:].rearrange("p (m t) -> p t m", t=PACK))
-            nc.vector.tensor_copy(words[:], ww_raw[:].rearrange("p (m t) -> p t m", t=PACK))
-            return words, scales
+        w2s = planes1[:, 2 * S : 3 * S]
 
-        w1w, w1s = deal("w1")
-        load_scales(w2_scales, [nc.sync] * QUADS)
-        nc.sync.dma_start(ww_raw[:], words_view(w2_words))
+        w1w = keep.tile([P, PACK, P], I32, name="w1w", align_bytes=64)
+        w2w = keep.tile([P, PACK, P], I32, name="w2w", align_bytes=64)
+        nc.vector.tensor_copy(w1w[:], dealt(w1w_raw))
 
         gain = keep.tile([P, PACK, W], F32, name="gain")
+        nc.scalar.activation(gain[:], gn_sb[:].unsqueeze(2).to_broadcast([P, PACK, W]), ACT.Copy)
 
         xw_picked = [keep.tile([P, HALF], U32, name=f"xw_picked{h}", align_bytes=64) for h in range(2)]
         for h in range(2):
@@ -98,7 +107,7 @@ def tile_picked_hashfillgate_none_po_kernel(
             nc.tensor.matmul_mx(
                 dst,
                 lhsT=words[:, t, :].bitcast(FP8X4),
-                lhsT_scale=scales[:, t, :],
+                lhsT_scale=scales[:, t * P : (t + 1) * P],
                 rhs=rhs_words.bitcast(FP8X4),
                 rhs_scale=rhs_scales,
                 start=True,
@@ -118,7 +127,7 @@ def tile_picked_hashfillgate_none_po_kernel(
                     if halves[h].start >= cols.start and halves[h].stop <= cols.stop:
                         lo = halves[h].start - cols.start
                         product(y_ps[t, i][:, lo : lo + HALF], w1w, w1s, t, xw_picked[h][:], xs_plane[:, halves[h]])
-        w2w, w2s = deal("w2")
+        nc.vector.tensor_copy(w2w[:], dealt(w2w_raw))
 
         def fetch_y(t):
             for i, cols in enumerate(pieces[t]):
@@ -127,15 +136,14 @@ def tile_picked_hashfillgate_none_po_kernel(
         def fetch_z(t):
             for i, cols in enumerate(pieces[t]):
                 nc.scalar.activation(z_sb[t][:, cols], y_ps[t, i][:], ACT.Copy, scale=gn_sb[:, t : t + 1])
-            nc.scalar.activation(gain[:, t, :], gn_sb[:, t : t + 1].to_broadcast([P, W]), ACT.Copy)
 
-        pa = {t: keep.tile([P, W], F32, name=f"pa{t}") for t in order}
-        pb = {t: keep.tile([P, W], F32, name=f"pb{t}") for t in order}
-        ra = {t: keep.tile([P, W], F32, name=f"ra{t}") for t in order}
+        pa = keep.tile([P, PACK, W], F32, name="pa")
+        pb = keep.tile([P, PACK, W], F32, name="pb")
+        ra = keep.tile([P, PACK, W], F32, name="ra")
         z_bf = [keep.tile([P, HALF, PACK], BF16, name=f"z_bf{h}", align_bytes=64) for h in range(2)]
 
         def fill(t):
-            nc.vector.tensor_tensor(z_sb[t][:].indirect(n1_sb[:]), ra[t][:], gain[:, t, :], ALU.mult)
+            nc.vector.tensor_tensor(z_sb[t][:].indirect(n1_sb[:]), ra[:, t, :], gain[:, t, :], ALU.mult)
             if t % 2:
                 nc.scalar.copy(z_sb[t - 1][:, S : 2 * S], z_sb[t][:])
             else:
@@ -150,21 +158,16 @@ def tile_picked_hashfillgate_none_po_kernel(
                         nc.scalar.copy(z_bf[h][:, SPLIT:HALF, t : t + 2], pair[:, HALF + SPLIT : S, :])
 
         SPLIT = 96
-        fetch_y(order[0])
-        for i, t in enumerate(order):
-            if i + 1 < PACK:
-                fetch_y(order[i + 1])
+        for t in order:
+            fetch_y(t)
+        for t in order:
             fetch_z(t)
-            nc.vector.tensor_copy(pa[t][:], y_sb[t][:].indirect(n1_sb[:]))
-            if i > 0:
-                prev = order[i - 1]
-                nc.vector.tensor_tensor(ra[prev][:], pa[prev][:], pb[prev][:], ALU.max)
-            nc.vector.tensor_copy(pb[t][:], y_sb[t][:].indirect(n2_sb[:]))
-            if i > 0 and i + 1 < PACK:
-                fill(order[i - 1])
-        nc.vector.tensor_tensor(ra[t][:], pa[t][:], pb[t][:], ALU.max)
-        fill(order[PACK - 2])
-        fill(order[PACK - 1])
+        for t in order:
+            nc.vector.tensor_copy(pa[:, t, :], y_sb[t][:].indirect(n1_sb[:]))
+            nc.vector.tensor_copy(pb[:, t, :], y_sb[t][:].indirect(n2_sb[:]))
+        nc.vector.tensor_tensor(ra[:], pa[:], pb[:], ALU.max)
+        for t in order:
+            fill(t)
 
         z_words = keep.tile([P, S], U32, name="z_words", align_bytes=64)
         z_scales = keep.tile([P, S], U8, name="z_scales", align_bytes=64)
@@ -178,21 +181,25 @@ def tile_picked_hashfillgate_none_po_kernel(
 
         h_sb = [keep.tile([P, S], F32, name=f"h_sb{t}") for t in range(PACK)]
         for t in range(PACK):
-            nc.vector.tensor_copy(h_sb[t][:], h_ps[t][:])
+            if t == 0:
+                nc.scalar.copy(h_sb[t][:], h_ps[t][:])
+            else:
+                nc.vector.tensor_copy(h_sb[t][:], h_ps[t][:])
 
         out_rows = out_0.rearrange("(p t) n -> p t n", t=PACK)
         o_scales = keep.tile([P, S], U8, name="o_scales", align_bytes=64)
+        o_sb = keep.tile([P, PACK, S], F32, name="o_sb")
         chunks = [(0, 256), (256, 384), (384, 512)]
         for c, (lo, hi) in enumerate(chunks):
             cols = slice(lo, hi)
-            o_sb = keep.tile([P, PACK, hi - lo], F32, name=f"o_sb{c}")
             for t in range(PACK):
-                gate = keep.tile([P, hi - lo], F32, name=f"gate{c}{t}")
+                gate = keep.tile([P, hi - lo], F32, name=f"gate{c}{t}", tag=f"gate{t}")
                 nc.scalar.activation(gate[:], h_sb[t][:].indirect(entries(n3_sb, lo, hi)), ACT.Sigmoid)
-                nc.vector.tensor_tensor(o_sb[:, t, :], h_ps[t][:, cols], gate[:], ALU.mult)
-            nc.sync.dma_start(out_rows[:, :, cols], o_sb[:])
+                nc.vector.tensor_tensor(o_sb[:, t, cols], h_ps[t][:, cols], gate[:], ALU.mult)
+            nc.sync.dma_start(out_rows[:, :, cols], o_sb[:, :, cols])
             o_bf = keep.tile([P, hi - lo, PACK], BF16, name=f"o_bf{c}", align_bytes=64)
-            nc.vector.tensor_copy(o_bf[:], o_sb[:].rearrange("p t n -> p n t"))
+            caster = nc.gpsimd if c + 1 < len(chunks) else nc.vector
+            caster.tensor_copy(o_bf[:], o_sb[:, :, cols].rearrange("p t n -> p n t"))
             o_words = keep.tile([P, hi - lo], I32, name=f"o_words{c}", align_bytes=64)
             nc.vector.quantize_mx(o_words[:].bitcast(FP8X4), o_scales[:, cols], o_bf[:].rearrange("p n t -> p (n t)"))
             nc.sync.dma_start(words_view(out_1)[:, cols], o_words[:])

@@ -46,7 +46,8 @@ def tile_picked_hashfillgate_none_po_kernel(
         w2s_raw = keep.tile([P, S], U8, name="w2s_raw", align_bytes=64)
         w1w_raw = keep.tile([P, S], I32, name="w1w_raw", align_bytes=64)
         w2w_raw = keep.tile([P, S], I32, name="w2w_raw", align_bytes=64)
-        planes1 = keep.tile([P, 3 * S], U8, name="planes1", align_bytes=64)
+        planes1 = keep.tile([P, 2 * S], U8, name="planes1", align_bytes=64)
+        plane2 = keep.tile([P, S], U8, name="plane2", align_bytes=64)
         gn_sb = keep.tile([P, PACK], F32, name="gn_sb")
         warm = keep.tile([P, 2], F32, name="warm")
 
@@ -55,18 +56,19 @@ def tile_picked_hashfillgate_none_po_kernel(
             return rows.unsqueeze(1).to_broadcast([16, 8, rows.shape[1]])
 
         nc.vector.memset(planes1[:].bitcast(I32), 0)
+        nc.vector.memset(plane2[:].bitcast(I32), 0)
         nc.vector.memset(warm[:, 0:1], 0.0)
 
         nc.sync.dma_start(w1s_raw[:].bitcast(I32), repeated(w1_scales))
-        nc.sync.dma_start(w2s_raw[:].bitcast(I32), repeated(w2_scales))
         nc.sync.dma_start(offs_sb[:], offs)
         nc.sync.dma_start(xs_table[:].bitcast(I32), repeated(x_scales))
         nc.sync.dma_start(n1_sb[:], n1)
         nc.sync.dma_start(n2_sb[:], n2)
         nc.sync.dma_start(gn_sb[:], gn.rearrange("(p t) o -> p (t o)", t=PACK))
+        nc.sync.dma_start(n3_sb[:], n3)
         nc.sync.dma_start(xw_table[:], words_view(x_words))
         nc.sync.dma_start(w1w_raw[:], words_view(w1_words))
-        nc.sync.dma_start(n3_sb[:], n3)
+        nc.sync.dma_start(w2s_raw[:].bitcast(I32), repeated(w2_scales))
         nc.sync.dma_start(w2w_raw[:], words_view(w2_words))
         nc.scalar.activation(warm[:, 1:2], warm[:, 0:1], ACT.Sigmoid)
 
@@ -77,21 +79,19 @@ def tile_picked_hashfillgate_none_po_kernel(
             for q in range(QUADS):
                 queues[q].dma_start(dst[32 * q : 32 * q + 4, :].bitcast(I32), src[32 * q : 32 * q + 32 : 8, :].bitcast(I32))
 
-        rows1 = keep.tile([P, 3 * S], U8, name="rows1", align_bytes=64)
+        rows1 = keep.tile([P, 2 * S], U8, name="rows1", align_bytes=64)
         nc.vector.tensor_copy(rows1[:, S : 2 * S].rearrange("p (t m) -> p t m", t=PACK), dealt(w1s_raw))
-        nc.gpsimd.tensor_copy(rows1[:, 2 * S : 3 * S].rearrange("p (t m) -> p t m", t=PACK), dealt(w2s_raw))
         xs_picked = keep.tile([P, S], U8, name="xs_picked", align_bytes=64)
         nc.vector.tensor_copy(xs_picked[:], xs_table[:].indirect(offs_sb[:]))
         nc.vector.tensor_copy(rows1[:, 0:S].bitcast(I32), xs_picked[:].bitcast(I32))
-        move_rows(planes1, rows1, [nc.sync, nc.scalar, nc.sync, nc.scalar])
+        move_rows(planes1, rows1, [nc.scalar] * QUADS)
         xs_plane = planes1[:, 0:S]
         w1s = planes1[:, S : 2 * S]
 
-        w2s = planes1[:, 2 * S : 3 * S]
+        w2s = plane2[:]
 
         w1w = keep.tile([P, PACK, P], I32, name="w1w", align_bytes=64)
         w2w = keep.tile([P, PACK, P], I32, name="w2w", align_bytes=64)
-        nc.vector.tensor_copy(w1w[:], dealt(w1w_raw))
 
         gain = keep.tile([P, PACK, W], F32, name="gain")
         nc.scalar.activation(gain[:], gn_sb[:].unsqueeze(2).to_broadcast([P, PACK, W]), ACT.Copy)
@@ -116,6 +116,8 @@ def tile_picked_hashfillgate_none_po_kernel(
 
         halves = [slice(0, HALF), slice(HALF, S)]
         order = (1, 3, 0, 2)
+        for t in order:
+            nc.vector.tensor_copy(w1w[:, t, :], dealt(w1w_raw)[:, t, :])
         y_sb = {t: keep.tile([P, S], F32, name=f"y_sb{t}") for t in order}
         z_sb = {t: keep.tile([P, S if t % 2 else 2 * S], F32, name=f"z_sb{t}") for t in order}
         pieces = {t: (halves if t == order[0] else [slice(0, S)]) for t in order}
@@ -127,6 +129,9 @@ def tile_picked_hashfillgate_none_po_kernel(
                     if halves[h].start >= cols.start and halves[h].stop <= cols.stop:
                         lo = halves[h].start - cols.start
                         product(y_ps[t, i][:, lo : lo + HALF], w1w, w1s, t, xw_picked[h][:], xs_plane[:, halves[h]])
+        rows2 = keep.tile([P, S], U8, name="rows2", align_bytes=64)
+        nc.vector.tensor_copy(rows2[:].rearrange("p (t m) -> p t m", t=PACK), dealt(w2s_raw))
+        move_rows(plane2, rows2, [nc.sync] * QUADS)
         nc.vector.tensor_copy(w2w[:], dealt(w2w_raw))
 
         def fetch_y(t):
@@ -171,18 +176,21 @@ def tile_picked_hashfillgate_none_po_kernel(
 
         z_words = keep.tile([P, S], U32, name="z_words", align_bytes=64)
         z_scales = keep.tile([P, S], U8, name="z_scales", align_bytes=64)
-        h_ps = [psum.tile([P, S], F32, name=f"h_ps{t}", tag=f"bank{(t + 5) % 8}") for t in range(PACK)]
+        h_ps = [psum.tile([P, S], F32, name=f"h_ps{t}", tag=f"bank{(t + 5) % 8}") if t else None for t in range(PACK)]
+        h0_ps = [psum.tile([P, HALF], F32, name=f"h0_ps{h}", tag=f"bank{4 + h}") for h in range(2)]
         for h in range(2):
             cols = halves[h]
             nc.vector.quantize_mx(z_words[:, cols].bitcast(FP8X4), z_scales[:, cols], z_bf[h][:].rearrange("p n t -> p (n t)"))
-            product(h_ps[0][:, cols], w2w, w2s, 0, z_words[:, cols], z_scales[:, cols])
-        for t in range(1, PACK):
+            product(h0_ps[h][:], w2w, w2s, 0, z_words[:, cols], z_scales[:, cols])
+            product(h_ps[1][:, cols], w2w, w2s, 1, z_words[:, cols], z_scales[:, cols])
+        for t in range(2, PACK):
             product(h_ps[t][:], w2w, w2s, t, z_words[:], z_scales[:])
 
         h_sb = [keep.tile([P, S], F32, name=f"h_sb{t}") for t in range(PACK)]
         for t in range(PACK):
             if t == 0:
-                nc.scalar.copy(h_sb[t][:], h_ps[t][:])
+                for h in range(2):
+                    nc.scalar.copy(h_sb[t][:, halves[h]], h0_ps[h][:])
             else:
                 nc.vector.tensor_copy(h_sb[t][:], h_ps[t][:])
 
@@ -195,11 +203,15 @@ def tile_picked_hashfillgate_none_po_kernel(
             for t in range(PACK):
                 gate = keep.tile([P, hi - lo], F32, name=f"gate{c}{t}", tag=f"gate{t}")
                 nc.scalar.activation(gate[:], h_sb[t][:].indirect(entries(n3_sb, lo, hi)), ACT.Sigmoid)
-                nc.vector.tensor_tensor(o_sb[:, t, cols], h_ps[t][:, cols], gate[:], ALU.mult)
+                nc.vector.tensor_tensor(o_sb[:, t, cols], h_ps[t][:, cols] if t else h0_ps[lo // HALF][:, lo % HALF : lo % HALF + hi - lo], gate[:], ALU.mult)
             nc.sync.dma_start(out_rows[:, :, cols], o_sb[:, :, cols])
             o_bf = keep.tile([P, hi - lo, PACK], BF16, name=f"o_bf{c}", align_bytes=64)
-            caster = nc.gpsimd if c + 1 < len(chunks) else nc.vector
-            caster.tensor_copy(o_bf[:], o_sb[:, :, cols].rearrange("p t n -> p n t"))
+            turned = o_sb[:, :, cols].rearrange("p t n -> p n t")
+            if c + 1 < len(chunks):
+                nc.vector.tensor_copy(o_bf[:], turned)
+            else:
+                nc.vector.tensor_copy(o_bf[:, 0:88, :], turned[:, 0:88, :])
+                nc.scalar.copy(o_bf[:, 88:128, :], turned[:, 88:128, :])
             o_words = keep.tile([P, hi - lo], I32, name=f"o_words{c}", align_bytes=64)
             nc.vector.quantize_mx(o_words[:].bitcast(FP8X4), o_scales[:, cols], o_bf[:].rearrange("p n t -> p (n t)"))
             nc.sync.dma_start(words_view(out_1)[:, cols], o_words[:])

from contextlib import ExitStack

import concourse.mybir as mybir

F32 = mybir.dt.float32
BF16 = mybir.dt.bfloat16
I32 = mybir.dt.int32
U32 = mybir.dt.uint32
U16 = mybir.dt.uint16
U8 = mybir.dt.uint8
FP8X4 = mybir.dt.float8_e4m3fn_x4
ALU = mybir.AluOpType
ACT = mybir.ActivationFunctionType

P = 128
PACK = 4
T = 2048
S = 512
W = 256
HALF = S // 2
QUADS = 4
FLOPS = 2 * 2 * 512 * 512 * 512


def tile_picked_hashfillgate_none_po_kernel(
    tc, x_words, x_scales, w1_words, w1_scales, gn, w2_words, w2_scales, offs, n1, n2, n3, out_0, out_1, out_2
):
    nc = tc.nc
    with ExitStack() as ctx:
        keep = ctx.enter_context(tc.tile_pool(name="keep", bufs=1))
        psum = ctx.enter_context(tc.psum_pool(name="psum", bufs=1))

        def words_view(dram):
            return dram[0].rearrange("p n r -> p (n r)").bitcast(I32)

        def entries(lst, lo, hi):
            return lst[:, lo // 16 : hi // 16]

        offs_sb = keep.tile([P, S // 16], U16, name="offs_sb")
        n1_sb = keep.tile([P, W // 16], U16, name="n1_sb")
        n2_sb = keep.tile([P, W // 16], U16, name="n2_sb")
        n3_sb = keep.tile([P, S // 16], U16, name="n3_sb")
        xs_table = keep.tile([P, T], U8, name="xs_table", align_bytes=64)
        xw_table = keep.tile([P, T], I32, name="xw_table", align_bytes=64)
        w1s_raw = keep.tile([P, S], U8, name="w1s_raw", align_bytes=64)
        w2s_raw = keep.tile([P, S], U8, name="w2s_raw", align_bytes=64)
        w1w_raw = keep.tile([P, S], I32, name="w1w_raw", align_bytes=64)
        w2w_raw = keep.tile([P, S], I32, name="w2w_raw", align_bytes=64)
        planes1 = keep.tile([P, 2 * S], U8, name="planes1", align_bytes=64)
        plane2 = keep.tile([P, S], U8, name="plane2", align_bytes=64)
        gn_sb = keep.tile([P, PACK], F32, name="gn_sb")
        warm = keep.tile([P, 2], F32, name="warm")

        def repeated(dram):
            rows = dram[0].bitcast(I32)
            return rows.unsqueeze(1).to_broadcast([16, 8, rows.shape[1]])

        nc.vector.memset(planes1[:].bitcast(I32), 0)
        nc.vector.memset(plane2[:].bitcast(I32), 0)
        nc.vector.memset(warm[:, 0:1], 0.0)

        nc.sync.dma_start(w1s_raw[:].bitcast(I32), repeated(w1_scales))
        nc.sync.dma_start(offs_sb[:], offs)
        nc.sync.dma_start(xs_table[:].bitcast(I32), repeated(x_scales))
        nc.sync.dma_start(n1_sb[:], n1)
        nc.sync.dma_start(n2_sb[:], n2)
        nc.sync.dma_start(gn_sb[:], gn.rearrange("(p t) o -> p (t o)", t=PACK))
        nc.sync.dma_start(n3_sb[:], n3)
        nc.sync.dma_start(xw_table[:], words_view(x_words))
        nc.sync.dma_start(w1w_raw[:], words_view(w1_words))
        nc.sync.dma_start(w2s_raw[:].bitcast(I32), repeated(w2_scales))
        nc.sync.dma_start(w2w_raw[:], words_view(w2_words))
        nc.scalar.activation(warm[:, 1:2], warm[:, 0:1], ACT.Sigmoid)

        def dealt(raw):
            return raw[:].rearrange("p (m t) -> p t m", t=PACK)

        def move_rows(dst, src, queues):
            for q in range(QUADS):
                queues[q].dma_start(dst[32 * q : 32 * q + 4, :].bitcast(I32), src[32 * q : 32 * q + 32 : 8, :].bitcast(I32))

        rows1 = keep.tile([P, 2 * S], U8, name="rows1", align_bytes=64)
        nc.vector.tensor_copy(rows1[:, S : 2 * S].rearrange("p (t m) -> p t m", t=PACK), dealt(w1s_raw))
        xs_picked = keep.tile([P, S], U8, name="xs_picked", align_bytes=64)
        nc.vector.tensor_copy(xs_picked[:], xs_table[:].indirect(offs_sb[:]))
        nc.vector.tensor_copy(rows1[:, 0:S].bitcast(I32), xs_picked[:].bitcast(I32))
        move_rows(planes1, rows1, [nc.scalar] * QUADS)
        xs_plane = planes1[:, 0:S]
        w1s = planes1[:, S : 2 * S]

        w2s = plane2[:]

        w1w = keep.tile([P, PACK, P], I32, name="w1w", align_bytes=64)
        w2w = keep.tile([P, PACK, P], I32, name="w2w", align_bytes=64)

        gain = keep.tile([P, PACK, W], F32, name="gain")
        nc.scalar.activation(gain[:], gn_sb[:].unsqueeze(2).to_broadcast([P, PACK, W]), ACT.Copy)

        xw_picked = [keep.tile([P, HALF], U32, name=f"xw_picked{h}", align_bytes=64) for h in range(2)]
        for h in range(2):
            nc.vector.tensor_copy(
                xw_picked[h][:],
                xw_table[:].bitcast(U32).indirect(entries(offs_sb, h * HALF, (h + 1) * HALF)),
            )

        def product(dst, words, scales, t, rhs_words, rhs_scales):
            nc.tensor.matmul_mx(
                dst,
                lhsT=words[:, t, :].bitcast(FP8X4),
                lhsT_scale=scales[:, t * P : (t + 1) * P],
                rhs=rhs_words.bitcast(FP8X4),
                rhs_scale=rhs_scales,
                start=True,
                stop=True,
            )

        halves = [slice(0, HALF), slice(HALF, S)]
        order = (1, 3, 0, 2)
        for t in order:
            nc.vector.tensor_copy(w1w[:, t, :], dealt(w1w_raw)[:, t, :])
        y_sb = {t: keep.tile([P, S], F32, name=f"y_sb{t}") for t in order}
        z_sb = {t: keep.tile([P, S if t % 2 else 2 * S], F32, name=f"z_sb{t}") for t in order}
        pieces = {t: (halves if t == order[0] else [slice(0, S)]) for t in order}
        y_ps = {}
        for t in order:
            for i, cols in enumerate(pieces[t]):
                y_ps[t, i] = psum.tile([P, cols.stop - cols.start], F32, name=f"y_ps{t}_{i}", tag=f"bank{t + 4 * i}")
                for h in range(2):
                    if halves[h].start >= cols.start and halves[h].stop <= cols.stop:
                        lo = halves[h].start - cols.start
                        product(y_ps[t, i][:, lo : lo + HALF], w1w, w1s, t, xw_picked[h][:], xs_plane[:, halves[h]])
        rows2 = keep.tile([P, S], U8, name="rows2", align_bytes=64)
        nc.vector.tensor_copy(rows2[:].rearrange("p (t m) -> p t m", t=PACK), dealt(w2s_raw))
        move_rows(plane2, rows2, [nc.sync] * QUADS)
        nc.vector.tensor_copy(w2w[:], dealt(w2w_raw))

        def fetch_y(t):
            for i, cols in enumerate(pieces[t]):
                nc.scalar.copy(y_sb[t][:, cols], y_ps[t, i][:])

        def fetch_z(t):
            for i, cols in enumerate(pieces[t]):
                nc.scalar.activation(z_sb[t][:, cols], y_ps[t, i][:], ACT.Copy, scale=gn_sb[:, t : t + 1])

        pa = keep.tile([P, PACK, W], F32, name="pa")
        pb = keep.tile([P, PACK, W], F32, name="pb")
        ra = keep.tile([P, PACK, W], F32, name="ra")
        z_bf = [keep.tile([P, HALF, PACK], BF16, name=f"z_bf{h}", align_bytes=64) for h in range(2)]

        def fill(t):
            nc.vector.tensor_tensor(z_sb[t][:].indirect(n1_sb[:]), ra[:, t, :], gain[:, t, :], ALU.mult)
            if t % 2:
                nc.scalar.copy(z_sb[t - 1][:, S : 2 * S], z_sb[t][:])
            else:
                pair = z_sb[t][:].rearrange("p (e n) -> p n e", e=2)
                for h in range(2):
                    if t == 0:
                        nc.scalar.copy(z_bf[h][:, :, t : t + 2], pair[:, halves[h], :])
                    elif h == 0:
                        nc.vector.tensor_copy(z_bf[h][:, :, t : t + 2], pair[:, halves[h], :])
                    else:
                        nc.vector.tensor_copy(z_bf[h][:, 0:SPLIT, t : t + 2], pair[:, HALF : HALF + SPLIT, :])
                        nc.scalar.copy(z_bf[h][:, SPLIT:HALF, t : t + 2], pair[:, HALF + SPLIT : S, :])

        SPLIT = 96
        for t in order:
            fetch_y(t)
        for t in order:
            fetch_z(t)
        for t in order:
            nc.vector.tensor_copy(pa[:, t, :], y_sb[t][:].indirect(n1_sb[:]))
            nc.vector.tensor_copy(pb[:, t, :], y_sb[t][:].indirect(n2_sb[:]))
        nc.vector.tensor_tensor(ra[:], pa[:], pb[:], ALU.max)
        for t in order:
            fill(t)

        z_words = keep.tile([P, S], U32, name="z_words", align_bytes=64)
        z_scales = keep.tile([P, S], U8, name="z_scales", align_bytes=64)
        h_ps = [psum.tile([P, S], F32, name=f"h_ps{t}", tag=f"bank{(t + 5) % 8}") if t else None for t in range(PACK)]
        h0_ps = [psum.tile([P, HALF], F32, name=f"h0_ps{h}", tag=f"bank{4 + h}") for h in range(2)]
        for h in range(2):
            cols = halves[h]
            nc.vector.quantize_mx(z_words[:, cols].bitcast(FP8X4), z_scales[:, cols], z_bf[h][:].rearrange("p n t -> p (n t)"))
            product(h0_ps[h][:], w2w, w2s, 0, z_words[:, cols], z_scales[:, cols])
            product(h_ps[1][:, cols], w2w, w2s, 1, z_words[:, cols], z_scales[:, cols])
        for t in range(2, PACK):
            product(h_ps[t][:], w2w, w2s, t, z_words[:], z_scales[:])

        h_sb = [keep.tile([P, S], F32, name=f"h_sb{t}") for t in range(PACK)]
        for t in range(PACK):
            if t == 0:
                for h in range(2):
                    nc.scalar.copy(h_sb[t][:, halves[h]], h0_ps[h][:])
            else:
                nc.vector.tensor_copy(h_sb[t][:], h_ps[t][:])

        out_rows = out_0.rearrange("(p t) n -> p t n", t=PACK)
        o_scales = keep.tile([P, S], U8, name="o_scales", align_bytes=64)
        o_sb = keep.tile([P, PACK, S], F32, name="o_sb")
        chunks = [(0, 256), (256, 384), (384, 512)]
        for c, (lo, hi) in enumerate(chunks):
            cols = slice(lo, hi)
            for t in range(PACK):
                gate = keep.tile([P, hi - lo], F32, name=f"gate{c}{t}", tag=f"gate{t}")
                nc.scalar.activation(gate[:], h_sb[t][:].indirect(entries(n3_sb, lo, hi)), ACT.Sigmoid)
                nc.vector.tensor_tensor(o_sb[:, t, cols], h_ps[t][:, cols] if t else h0_ps[lo // HALF][:, lo % HALF : lo % HALF + hi - lo], gate[:], ALU.mult)
            nc.sync.dma_start(out_rows[:, :, cols], o_sb[:, :, cols])
            o_bf = keep.tile([P, hi - lo, PACK], BF16, name=f"o_bf{c}", align_bytes=64)
            turned = o_sb[:, :, cols].rearrange("p t n -> p n t")
            if c + 1 < len(chunks):
                nc.vector.tensor_copy(o_bf[:], turned)
            else:
                nc.vector.tensor_copy(o_bf[:, 0:88, :], turned[:, 0:88, :])
                nc.scalar.copy(o_bf[:, 88:128, :], turned[:, 88:128, :])
            o_words = keep.tile([P, hi - lo], I32, name=f"o_words{c}", align_bytes=64)
            nc.vector.quantize_mx(o_words[:].bitcast(FP8X4), o_scales[:, cols], o_bf[:].rearrange("p n t -> p (n t)"))
            nc.sync.dma_start(words_view(out_1)[:, cols], o_words[:])
        for q in range(QUADS):
            queue = nc.sync if q % 2 == 0 else nc.scalar
            queue.dma_start(out_2[0, 4 * q : 4 * q + 4, :].bitcast(I32), o_scales[32 * q : 32 * q + 4, :].bitcast(I32))
